import numpy as np
import ml_dtypes


def mxq(x, axis, fmt="e4m3"):
    dtype, down = {"e4m3": (ml_dtypes.float8_e4m3fn, 7), "e5m2": (ml_dtypes.float8_e5m2, 14)}[fmt]
    v = np.moveaxis(np.asarray(x, np.float32).astype(ml_dtypes.bfloat16).astype(np.float64), axis, -1)
    blocks = v.reshape(v.shape[:-1] + (-1, 32))
    amax = np.abs(blocks).max(-1, keepdims=True)
    byte = np.maximum(np.where(amax > 0, np.frexp(amax)[1] - 1 + 127, 0) - down, 1)
    scale = np.exp2(byte - 127.0)
    codes = (blocks / scale).astype(np.float32).astype(dtype).astype(np.float64)
    return np.moveaxis((codes * scale).reshape(v.shape), -1, axis)


WIDE = False


def mx_kscale(k):
    if not WIDE:
        return np.ones(k)
    levels = np.array([10, -10, 5, -5, 0])
    if k % 512:
        return np.exp2(np.random.permutation(np.resize(levels, k // 32))).repeat(32)
    a = np.empty((k // 512, 16))
    for p in range(k // 512):
        a[p, :8] = np.random.permutation(np.resize(levels, 8))
        for g in range(8):
            far = levels[np.abs(levels - a[p, g]) >= 10]
            a[p, g + 8] = far[np.random.randint(len(far))]
    return np.exp2(a.ravel()).repeat(32)


def f64(x):
    return np.asarray(x).astype(np.float64)


def striped(idx):
    return np.tile(idx.reshape(-1, 16).T, (8, 1)).astype(np.uint16)


def unstriped(offs):
    return offs[:16].T.reshape(-1).astype(np.int64)


E2M1 = np.array([0.0, 0.5, 1.0, 1.5, 2.0, 3.0, 4.0, 6.0, -0.0, -0.5, -1.0, -1.5, -2.0, -3.0, -4.0, -6.0])


def pack_weight(w, fmt):
    k, n = w.shape
    w = f64(np.asarray(w, np.float32).astype(ml_dtypes.bfloat16)).reshape(k // 32, 32, n)
    amax = np.abs(w).max(1)
    if fmt == "e4m3":
        byte = np.frexp(amax)[1] - 1 + 127 - 7
    else:
        mant, ex = np.frexp(amax / 6.0)
        byte = np.where(mant > 0.5, ex, ex - 1) + 127
    byte = np.clip(np.where(amax > 0, byte, 1), 1, 254)
    scaled = (w * np.exp2(127.0 - byte)[:, None, :]).reshape(k, n).astype(np.float32)
    by_word = np.ascontiguousarray(scaled.reshape(k // 512, 128, 4, n).transpose(0, 1, 3, 2))
    if fmt == "e4m3":
        words = by_word.astype(ml_dtypes.float8_e4m3fn).view(np.uint8)
    else:
        c = by_word.astype(ml_dtypes.float4_e2m1fn).view(np.uint8) & 0xF
        words = (c[..., 0::2] | (c[..., 1::2] << 4)).reshape(k // 512, 128, 2 * n)
    return np.ascontiguousarray(words), np.ascontiguousarray(byte.astype(np.uint8).reshape(k // 512, 16, n))


def unpack_weight(words, scales, fmt):
    g, _, n = scales.shape
    words = np.ascontiguousarray(words).reshape(g, 128, n, -1)
    if fmt == "e4m3":
        vals = words.view(ml_dtypes.float8_e4m3fn).astype(np.float64)
    else:
        nib = np.empty((g, 128, n, 4), np.uint8)
        nib[..., 0::2] = words & 0xF
        nib[..., 1::2] = words >> 4
        vals = E2M1[nib]
    vals = vals * np.repeat(np.exp2(scales.astype(np.float64) - 127.0), 8, axis=1)[..., None]
    return vals.transpose(0, 1, 3, 2).reshape(g * 512, n)


def gelu(v):
    return 0.5 * v * (1.0 + np.tanh(np.sqrt(2.0 / np.pi) * (v + 0.044715 * v**3)))


def striped8(idx):
    return np.concatenate([v.reshape(-1, 16).T for v in idx]).astype(np.uint16)


def unstriped8(offs):
    return np.stack([offs[16 * g:16 * g + 16].T.reshape(-1) for g in range(8)]).astype(np.int64)


def heads(h, wgt, idx8):
    r = np.arange(h.shape[0])
    return wgt[r // 4 % 128] * h[r[:, None], idx8[r % 512 // 64]]


def put_heads(h, wgs, idx8, t2):
    r = np.arange(h.shape[0])
    page = np.zeros((h.shape[0], t2))
    page[r[:, None], idx8[r % 512 // 64]] = wgs[r // 4 % 128] * h
    return page


K, T, S, P, T2, H, N = 1536, 2048, 1024, 1024, 2048, 512, 640


def setup_inputs():
    n = np.random.standard_normal
    s = mx_kscale(K)[:, None]
    u = mx_kscale(H)[:, None]
    d = {}
    d["tab_words"], d["tab_scales"] = pack_weight(n((K, T)) * s, "e4m3")
    d["offs"] = striped(np.random.permutation(T)[:S])
    d["offs2"] = striped8(np.stack([np.random.permutation(T2)[:S] for _ in range(8)]))
    d["offs3"] = striped8(np.stack([np.random.permutation(T2)[:P] for _ in range(8)]))
    d["w1"] = (n((K, H)) / s / K**0.5).astype(np.float32)
    d["cartoon"] = n((H, S)).astype(np.float32)
    d["gain"] = (np.random.choice([-1.0, 1.0], H) * np.random.uniform(0.6, 1.4, H) * u[:, 0]).astype(np.float32)
    d["wgs"] = np.repeat(np.random.uniform(0.5, 2.0, (8, S)), 16, axis=0).astype(np.float32)
    d["wgt"] = np.repeat(np.random.uniform(0.5, 2.0, (8, P)), 16, axis=0).astype(np.float32)
    d["pile"] = ((0.5 + n((H, P))) * u).astype(np.float32)
    d["wd_words"], d["wd_scales"] = pack_weight(0.8 * n((H, N)) / u / H**0.5, "e2m1")
    d["wt"] = (1.2 * n((H, N)) / u / H**0.5).astype(np.float32)
    d["bias"] = (0.5 * n(N)).astype(np.float32)
    return d


def reference(tab_words, tab_scales, offs, offs2, offs3, w1, cartoon, gain, wgs, wgt, pile, wd_words, wd_scales, wt, bias):
    v = unpack_weight(tab_words, tab_scales, "e4m3")[:, unstriped(offs)]
    knots = mxq(f64(w1), 0, "e4m3").T @ v
    h = f64(gain)[:, None] * np.abs(knots - f64(cartoon))
    page = put_heads(h, f64(wgs), unstriped8(offs2), T2)
    x = heads(page, f64(wgt), unstriped8(offs3))
    z = mxq(np.minimum(x, f64(pile)), 0, "e4m3")
    wd = unpack_weight(wd_words, wd_scales, "e2m1")
    density = wd.T @ z
    pattern = mxq(f64(wt), 0, "e4m3").T @ z
    return density + np.tanh(pattern + f64(bias)[:, None])

@@ -1,0 +1,256 @@
+from contextlib import ExitStack
+
+import concourse.mybir as mybir
+from concourse.masks import make_identity
+
+K, T, S, M, T2, H, N = 1536, 2048, 1024, 1024, 2048, 512, 640
+FLOPS = 2 * K * H * S + 2 * 2 * H * N * M
+
+F32 = mybir.dt.float32
+BF16 = mybir.dt.bfloat16
+I32 = mybir.dt.int32
+U32 = mybir.dt.uint32
+U16 = mybir.dt.uint16
+U8 = mybir.dt.uint8
+E4M3X4 = mybir.dt.float8_e4m3fn_x4
+E2M1X4 = mybir.dt.float4_e2m1fn_x4
+ALU = mybir.AluOpType
+ACT = mybir.ActivationFunctionType
+
+P = 128
+PACK = 4
+PASSES = K // (P * PACK)
+BANK = 512
+LIST_ROWS = 16
+N_TILES = N // P
+SCALAR_SHARE = (128, 128, 76)
+
+
+def tile_list_knot_density_checks_kernel(
+    tc, tab_words, tab_scales, offs, offs2, offs3, w1, cartoon, gain, wgs, wgt, pile, wd_words, wd_scales, wt, bias, out
+):
+    nc = tc.nc
+
+    def entries(list_tile, a, b):
+        return list_tile[:, a // LIST_ROWS : b // LIST_ROWS]
+
+    with ExitStack() as ctx:
+        lists = ctx.enter_context(tc.tile_pool(name="lists", bufs=1))
+        keep = ctx.enter_context(tc.tile_pool(name="keep", bufs=1))
+        ring = ctx.enter_context(tc.tile_pool(name="ring", bufs=2))
+        psum = ctx.enter_context(tc.psum_pool(name="psum", bufs=4))
+
+        idx = lists.tile([P, S // LIST_ROWS], U16, name="idx")
+        idx2 = lists.tile([P, S // LIST_ROWS], U16, name="idx2")
+        idx3 = lists.tile([P, M // LIST_ROWS], U16, name="idx3")
+
+        tab_sc = keep.tile([P, T], U8, name="tab_sc", align_bytes=64)
+        wd_sc = keep.tile([P, N], U8, name="wd_sc", align_bytes=64)
+        pages = [keep.tile([P, T2], F32, name=f"page{u}") for u in range(2)]
+        ident = keep.tile([P, P], F32, name="ident")
+        tab_sc_rows = keep.tile([P, T // 4], I32, name="tab_sc_rows")
+
+        def load_tab_scales(queue, q):
+            queue.dma_start(
+                out=tab_sc_rows[32 * q : 32 * q + 4 * PASSES, :],
+                in_=tab_scales[:, 4 * q : 4 * q + 4, :].bitcast(I32),
+            )
+
+        nc.vector.memset(tab_sc[:].bitcast(I32), 0)
+        nc.vector.memset(wd_sc[:].bitcast(I32), 0)
+        nc.vector.memset(pages[0][:], 0.0)
+        nc.gpsimd.memset(pages[1][:], 0.0)
+        make_identity(nc, ident[:])
+
+        tab = [keep.tile([P, T], U32, name=f"tab{a}") for a in range(PASSES)]
+        w1_raw = [keep.tile([P, PACK, H], F32, name=f"w1_raw{a}") for a in range(PASSES)]
+        gain_sb = keep.tile([P, PACK], F32, name="gain_sb")
+        bias_sb = keep.tile([P, N_TILES], F32, name="bias_sb")
+        cart = [keep.tile([P, S], F32, name=f"cart{i}") for i in range(PACK)]
+        wgs_sb = keep.tile([P, S], F32, name="wgs_sb")
+        wgt_sb = keep.tile([P, M], F32, name="wgt_sb")
+        halves = [(0, BANK), (BANK, 2 * BANK)]
+        pile_sb = [keep.tile([P, PACK, BANK], F32, name=f"pile{c}") for c in range(2)]
+        wt_raw = keep.tile([P, PACK, N], F32, name="wt_raw")
+        wd_codes = keep.tile([P, 2 * N], U8, name="wd_codes", align_bytes=64)
+
+        def load_w1(a):
+            rows = w1[a * P * PACK : (a + 1) * P * PACK, :]
+            nc.sync.dma_start(out=w1_raw[a][:], in_=rows.rearrange("(p j) c -> p j c", j=PACK))
+
+        def load_tab(a):
+            nc.sync.dma_start(out=tab[a][:].bitcast(I32), in_=tab_words[a].rearrange("p t i -> p (t i)").bitcast(I32))
+
+        cart_rows = cartoon.rearrange("(p i) j -> p i j", i=PACK)
+        pile_rows = pile.rearrange("(p i) m -> p i m", i=PACK)
+
+        nc.sync.dma_start(idx[:], offs)
+        load_tab_scales(nc.scalar, 2)
+        load_tab_scales(nc.scalar, 3)
+        load_tab(0)
+        load_tab_scales(nc.sync, 0)
+        load_tab_scales(nc.sync, 1)
+        load_w1(0)
+        load_w1(1)
+        load_tab(1)
+        nc.sync.dma_start(out=gain_sb[:], in_=gain.rearrange("(p i) -> p i", i=PACK))
+        nc.sync.dma_start(idx2[:], offs2)
+        load_w1(2)
+        load_tab(2)
+        for a, b in halves:
+            nc.sync.dma_start(out=cart[0][:, a:b], in_=cart_rows[:, 0, a:b])
+            nc.sync.dma_start(out=wgs_sb[:, a:b], in_=wgs[:, a:b])
+        nc.sync.dma_start(out=cart[1][:], in_=cart_rows[:, 1, :])
+        nc.sync.dma_start(idx3[:], offs3)
+        nc.sync.dma_start(out=wgt_sb[:], in_=wgt)
+        for i in range(2, PACK):
+            nc.sync.dma_start(out=cart[i][:], in_=cart_rows[:, i, :])
+        nc.sync.dma_start(out=wt_raw[:], in_=wt.rearrange("(p j) n -> p j n", j=PACK))
+        for c, (a, b) in enumerate(halves):
+            nc.sync.dma_start(out=pile_sb[c][:], in_=pile_rows[:, :, a:b])
+        nc.sync.dma_start(out=wd_codes[:].bitcast(I32), in_=wd_words[0].bitcast(I32))
+        for q in range(4):
+            nc.sync.dma_start(
+                out=wd_sc[32 * q : 32 * q + 4, :].bitcast(I32), in_=wd_scales[0, 4 * q : 4 * q + 4, :].bitcast(I32)
+            )
+        with nc.allow_non_contiguous_dma(reason="one bias value for each partition and tile of 128 rows"):
+            nc.sync.dma_start(out=bias_sb[:], in_=bias.rearrange("(c p) -> p c", p=P))
+
+        v_codes = [keep.tile([P, S], U32, name=f"v_codes{a}", align_bytes=64) for a in range(PASSES - 1)]
+        v_sc = keep.tile([P, S], U8, name="v_sc", align_bytes=64)
+        w1_codes = [keep.tile([P, H], U32, name=f"w1_codes{a}", align_bytes=64) for a in range(PASSES)]
+        w1_sc = [keep.tile([P, H], U8, name=f"w1_sc{a}", align_bytes=64) for a in range(PASSES)]
+
+        nc.vector.tensor_copy(v_codes[0][:], tab[0][:].indirect(idx[:]))
+        for q in range(4):
+            live = slice(32 * q, 32 * q + 4 * PASSES)
+            nc.vector.tensor_copy(tab_sc[live, :].bitcast(I32), tab_sc_rows[live, :])
+        nc.vector.tensor_copy(v_sc[:], tab_sc[:].indirect(idx[:]))
+        for a in range(PASSES):
+            grouped = keep.tile([P, H * PACK], BF16, name=f"w1_grouped{a}", align_bytes=64)
+            dst = grouped[:].rearrange("p (i m j) -> p m j i", i=PACK, j=PACK)
+            src = w1_raw[a][:].rearrange("p j (m i) -> p m j i", i=PACK)
+            share = SCALAR_SHARE[a]
+            nc.scalar.copy(out=dst[:, :share], in_=src[:, :share])
+            if share < P:
+                nc.vector.tensor_copy(out=dst[:, share:], in_=src[:, share:])
+            nc.vector.quantize_mx(out=w1_codes[a][:].bitcast(E4M3X4), scales=w1_sc[a][:], in_=grouped[:])
+            if a == 0:
+                nc.vector.tensor_copy(v_codes[1][:], tab[1][:].indirect(idx[:]))
+        v_codes.append(keep.tile([P, S], U32, name="v_codes2", tag="w1_grouped2", align_bytes=64))
+        for c0, c1 in halves:
+            nc.vector.tensor_copy(v_codes[2][:, c0:c1], tab[2][:].indirect(entries(idx, c0, c1)))
+
+        def knots(i, c0, c1):
+            acc = psum.tile([P, BANK], F32, name="acc")
+            for a in range(PASSES):
+                nc.tensor.matmul_mx(
+                    out=acc[:, : c1 - c0],
+                    lhsT=w1_codes[a][:, i * P : (i + 1) * P].bitcast(E4M3X4),
+                    lhsT_scale=w1_sc[a][:, i * P : (i + 1) * P],
+                    rhs=v_codes[a][:, c0:c1].bitcast(E4M3X4),
+                    rhs_scale=v_sc[4 * a :, c0:c1],
+                    start=(a == 0),
+                    stop=(a == PASSES - 1),
+                )
+            return acc[:, : c1 - c0]
+
+        def deviation_on_vector(h, i, c0, c1):
+            acc = knots(i, c0, c1)
+            diff = ring.tile([P, BANK], F32, name="stage_a")
+            nc.vector.tensor_tensor(diff[:, : c1 - c0], acc, cart[i][:, c0:c1], ALU.subtract)
+            size = ring.tile([P, BANK], F32, name="stage_b")
+            nc.scalar.activation(out=size[:, : c1 - c0], in_=diff[:, : c1 - c0], func=ACT.Abs)
+            nc.scalar.activation(out=h[:, c0:c1], in_=size[:, : c1 - c0], func=ACT.Copy, scale=gain_sb[:, i : i + 1])
+
+        def deviation_on_tensor(h, i, c0, c1):
+            acc = knots(i, c0, c1)
+            blocks = range((c1 - c0) // P)
+            negated = ring.tile([P, BANK], F32, name="stage_a")
+            nc.scalar.activation(out=negated[:], in_=acc, func=ACT.Copy, scale=-1.0)
+            turned = psum.tile([P, BANK], F32, name="turn")
+            for b in blocks:
+                nc.tensor.matmul(
+                    turned[:, b * P : (b + 1) * P], negated[:, b * P : (b + 1) * P], ident[:],
+                    start=True, stop=False, is_transpose=True,
+                )
+                nc.tensor.matmul(
+                    turned[:, b * P : (b + 1) * P], cart[i][:, c0 + b * P : c0 + (b + 1) * P], ident[:],
+                    start=False, stop=True, is_transpose=True,
+                )
+            size = ring.tile([P, BANK], F32, name="stage_b")
+            nc.scalar.activation(out=size[:], in_=turned[:], func=ACT.Abs)
+            back = psum.tile([P, BANK], F32, name="turn")
+            for b in blocks:
+                nc.tensor.transpose(back[:, b * P : (b + 1) * P], size[:, b * P : (b + 1) * P], ident[:])
+            nc.scalar.activation(out=h[:, c0:c1], in_=back[:], func=ACT.Copy, scale=gain_sb[:, i : i + 1])
+
+        x = [keep.tile([P, PACK, BANK], F32, name=f"x{c}") for c in range(2)]
+        for i in range(PACK):
+            h = keep.tile([P, S], F32, name=f"h{i}", align_bytes=64)
+            page = pages[i % 2]
+            if i == 0:
+                pieces = [(0, 256), (256, 512), (512, 1024)]
+                for c0, c1 in pieces:
+                    deviation_on_vector(h, i, c0, c1)
+            else:
+                pieces = halves if i == 1 else [(0, S)]
+                for c0, c1 in halves:
+                    deviation_on_tensor(h, i, c0, c1)
+            for c0, c1 in pieces:
+                nc.vector.tensor_tensor(page[:].indirect(entries(idx2, c0, c1)), h[:, c0:c1], wgs_sb[:, c0:c1], ALU.mult)
+            for c, (c0, c1) in enumerate(halves):
+                nc.vector.tensor_tensor(x[c][:, i, :], page[:].indirect(entries(idx3, c0, c1)), wgt_sb[:, c0:c1], ALU.mult)
+
+        wt_grouped = keep.tile([P, N * PACK], BF16, name="wt_grouped", tag="h3", align_bytes=64)
+        nc.scalar.copy(
+            out=wt_grouped[:].rearrange("p (c e j) -> p c j e", e=4, j=PACK),
+            in_=wt_raw[:].rearrange("p j (c e) -> p c j e", e=4),
+        )
+        wt_codes = keep.tile([P, N], U32, name="wt_codes", align_bytes=64)
+        wt_sc = keep.tile([P, N], U8, name="wt_sc", align_bytes=64)
+        for n0, n1 in ((0, BANK), (BANK, N)):
+            nc.vector.quantize_mx(
+                out=wt_codes[:, n0:n1].bitcast(E4M3X4), scales=wt_sc[:, n0:n1], in_=wt_grouped[:, PACK * n0 : PACK * n1]
+            )
+
+        z_codes, z_sc = [], []
+        for c in range(2):
+            z = ring.tile([P, BANK * PACK], BF16, name="z", align_bytes=64)
+            nc.vector.tensor_tensor(
+                z[:].rearrange("p (c e i) -> p c i e", e=4, i=PACK),
+                x[c][:].rearrange("p i (c e) -> p c i e", e=4),
+                pile_sb[c][:].rearrange("p i (c e) -> p c i e", e=4),
+                ALU.min,
+            )
+            z_codes.append(ring.tile([P, BANK], U32, name="z_codes", align_bytes=64))
+            z_sc.append(ring.tile([P, BANK], U8, name="z_sc", align_bytes=64))
+            nc.vector.quantize_mx(out=z_codes[c][:].bitcast(E4M3X4), scales=z_sc[c][:], in_=z[:])
+
+        for c, (c0, c1) in enumerate(halves):
+            for n in range(N_TILES):
+                pattern = psum.tile([P, BANK], F32, name="turn")
+                nc.tensor.matmul_mx(
+                    out=pattern[:],
+                    lhsT=wt_codes[:, n * P : (n + 1) * P].bitcast(E4M3X4),
+                    lhsT_scale=wt_sc[:, n * P : (n + 1) * P],
+                    rhs=z_codes[c][:].bitcast(E4M3X4),
+                    rhs_scale=z_sc[c][:],
+                    start=True,
+                    stop=True,
+                )
+                density = psum.tile([P, BANK], F32, name="acc")
+                nc.tensor.matmul_mx(
+                    out=density[:],
+                    lhsT=wd_codes[:, 2 * n * P : 2 * (n + 1) * P].bitcast(E2M1X4),
+                    lhsT_scale=wd_sc[:, n * P : (n + 1) * P],
+                    rhs=z_codes[c][:].bitcast(E4M3X4),
+                    rhs_scale=z_sc[c][:],
+                    start=True,
+                    stop=True,
+                )
+                bent = ring.tile([P, BANK], F32, name="bent", bufs=5)
+                nc.scalar.activation(out=bent[:], in_=pattern[:], func=ACT.Tanh, bias=bias_sb[:, n : n + 1])
+                result = ring.tile([P, BANK], F32, name="result", bufs=4)
+                nc.vector.tensor_tensor(result[:], density[:], bent[:], ALU.add)
+                nc.sync.dma_start(out=out[n * P : (n + 1) * P, c0:c1], in_=result[:])

@@ -38,7 +38,7 @@ def tile_list_knot_density_checks_kernel(
         lists = ctx.enter_context(tc.tile_pool(name="lists", bufs=1))
         keep = ctx.enter_context(tc.tile_pool(name="keep", bufs=1))
         ring = ctx.enter_context(tc.tile_pool(name="ring", bufs=2))
-        psum = ctx.enter_context(tc.psum_pool(name="psum", bufs=4))
+        psum = ctx.enter_context(tc.psum_pool(name="psum", bufs=3))
 
         idx = lists.tile([P, S // LIST_ROWS], U16, name="idx")
         idx2 = lists.tile([P, S // LIST_ROWS], U16, name="idx2")
@@ -142,7 +142,7 @@ def tile_list_knot_density_checks_kernel(
             nc.vector.tensor_copy(v_codes[2][:, c0:c1], tab[2][:].indirect(entries(idx, c0, c1)))
 
         def knots(i, c0, c1):
-            acc = psum.tile([P, BANK], F32, name="acc")
+            acc = psum.tile([P, BANK], F32, name="acc", bufs=5)
             for a in range(PASSES):
                 nc.tensor.matmul_mx(
                     out=acc[:, : c1 - c0],
@@ -190,8 +190,8 @@ def tile_list_knot_density_checks_kernel(
             h = keep.tile([P, S], F32, name=f"h{i}", align_bytes=64)
             page = pages[i % 2]
             if i == 0:
-                pieces = [(0, 256), (256, 512), (512, 1024)]
-                for c0, c1 in pieces:
+                pieces = [(0, 256), (256, 1024)]
+                for c0, c1 in [(0, 256), (256, 512), (512, 1024)]:
                     deviation_on_vector(h, i, c0, c1)
             else:
                 pieces = halves if i == 1 else [(0, S)]
@@ -227,30 +227,38 @@ def tile_list_knot_density_checks_kernel(
             z_sc.append(ring.tile([P, BANK], U8, name="z_sc", align_bytes=64))
             nc.vector.quantize_mx(out=z_codes[c][:].bitcast(E4M3X4), scales=z_sc[c][:], in_=z[:])
 
-        for c, (c0, c1) in enumerate(halves):
-            for n in range(N_TILES):
-                pattern = psum.tile([P, BANK], F32, name="turn")
-                nc.tensor.matmul_mx(
-                    out=pattern[:],
-                    lhsT=wt_codes[:, n * P : (n + 1) * P].bitcast(E4M3X4),
-                    lhsT_scale=wt_sc[:, n * P : (n + 1) * P],
-                    rhs=z_codes[c][:].bitcast(E4M3X4),
-                    rhs_scale=z_sc[c][:],
-                    start=True,
-                    stop=True,
-                )
-                density = psum.tile([P, BANK], F32, name="acc")
-                nc.tensor.matmul_mx(
-                    out=density[:],
-                    lhsT=wd_codes[:, 2 * n * P : 2 * (n + 1) * P].bitcast(E2M1X4),
-                    lhsT_scale=wd_sc[:, n * P : (n + 1) * P],
-                    rhs=z_codes[c][:].bitcast(E4M3X4),
-                    rhs_scale=z_sc[c][:],
-                    start=True,
-                    stop=True,
-                )
-                bent = ring.tile([P, BANK], F32, name="bent", bufs=5)
-                nc.scalar.activation(out=bent[:], in_=pattern[:], func=ACT.Tanh, bias=bias_sb[:, n : n + 1])
-                result = ring.tile([P, BANK], F32, name="result", bufs=4)
-                nc.vector.tensor_tensor(result[:], density[:], bent[:], ALU.add)
-                nc.sync.dma_start(out=out[n * P : (n + 1) * P, c0:c1], in_=result[:])
+        def bend(c, n):
+            pattern = psum.tile([P, BANK], F32, name="turn")
+            nc.tensor.matmul_mx(
+                out=pattern[:],
+                lhsT=wt_codes[:, n * P : (n + 1) * P].bitcast(E4M3X4),
+                lhsT_scale=wt_sc[:, n * P : (n + 1) * P],
+                rhs=z_codes[c][:].bitcast(E4M3X4),
+                rhs_scale=z_sc[c][:],
+                start=True,
+                stop=True,
+            )
+            result = ring.tile([P, BANK], F32, name="result", bufs=2 * N_TILES)
+            nc.scalar.activation(out=result[:], in_=pattern[:], func=ACT.Tanh, bias=bias_sb[:, n : n + 1])
+            return result
+
+        def finish(c, n, result):
+            density = psum.tile([P, BANK], F32, name="acc", bufs=5)
+            nc.tensor.matmul_mx(
+                out=density[:],
+                lhsT=wd_codes[:, 2 * n * P : 2 * (n + 1) * P].bitcast(E2M1X4),
+                lhsT_scale=wd_sc[:, n * P : (n + 1) * P],
+                rhs=z_codes[c][:].bitcast(E4M3X4),
+                rhs_scale=z_sc[c][:],
+                start=True,
+                stop=True,
+            )
+            nc.vector.tensor_tensor(result[:], density[:], result[:], ALU.add)
+            c0, c1 = halves[c]
+            nc.sync.dma_start(out=out[n * P : (n + 1) * P, c0:c1], in_=result[:])
+
+        results = [bend(0, n) for n in range(N_TILES)]
+        for n in range(N_TILES):
+            finish(0, n, results[n])
+        for n in range(N_TILES):
+            finish(1, n, bend(1, n))

from contextlib import ExitStack

import concourse.mybir as mybir
from concourse.masks import make_identity

K, T, S, M, T2, H, N = 1536, 2048, 1024, 1024, 2048, 512, 640
FLOPS = 2 * K * H * S + 2 * 2 * H * N * M

F32 = mybir.dt.float32
BF16 = mybir.dt.bfloat16
I32 = mybir.dt.int32
U32 = mybir.dt.uint32
U16 = mybir.dt.uint16
U8 = mybir.dt.uint8
E4M3X4 = mybir.dt.float8_e4m3fn_x4
E2M1X4 = mybir.dt.float4_e2m1fn_x4
ALU = mybir.AluOpType
ACT = mybir.ActivationFunctionType

P = 128
PACK = 4
PASSES = K // (P * PACK)
BANK = 512
LIST_ROWS = 16
N_TILES = N // P
SCALAR_SHARE = (128, 128, 76)


def tile_list_knot_density_checks_kernel(
    tc, tab_words, tab_scales, offs, offs2, offs3, w1, cartoon, gain, wgs, wgt, pile, wd_words, wd_scales, wt, bias, out
):
    nc = tc.nc

    def entries(list_tile, a, b):
        return list_tile[:, a // LIST_ROWS : b // LIST_ROWS]

    with ExitStack() as ctx:
        lists = ctx.enter_context(tc.tile_pool(name="lists", bufs=1))
        keep = ctx.enter_context(tc.tile_pool(name="keep", bufs=1))
        ring = ctx.enter_context(tc.tile_pool(name="ring", bufs=2))
        psum = ctx.enter_context(tc.psum_pool(name="psum", bufs=3))

        idx = lists.tile([P, S // LIST_ROWS], U16, name="idx")
        idx2 = lists.tile([P, S // LIST_ROWS], U16, name="idx2")
        idx3 = lists.tile([P, M // LIST_ROWS], U16, name="idx3")

        tab_sc = keep.tile([P, T], U8, name="tab_sc", align_bytes=64)
        wd_sc = keep.tile([P, N], U8, name="wd_sc", align_bytes=64)
        pages = [keep.tile([P, T2], F32, name=f"page{u}") for u in range(2)]
        ident = keep.tile([P, P], F32, name="ident")
        tab_sc_rows = keep.tile([P, T // 4], I32, name="tab_sc_rows")

        def load_tab_scales(queue, q):
            queue.dma_start(
                out=tab_sc_rows[32 * q : 32 * q + 4 * PASSES, :],
                in_=tab_scales[:, 4 * q : 4 * q + 4, :].bitcast(I32),
            )

        nc.vector.memset(tab_sc[:].bitcast(I32), 0)
        nc.vector.memset(wd_sc[:].bitcast(I32), 0)
        nc.vector.memset(pages[0][:], 0.0)
        nc.gpsimd.memset(pages[1][:], 0.0)
        make_identity(nc, ident[:])

        tab = [keep.tile([P, T], U32, name=f"tab{a}") for a in range(PASSES)]
        w1_raw = [keep.tile([P, PACK, H], F32, name=f"w1_raw{a}") for a in range(PASSES)]
        gain_sb = keep.tile([P, PACK], F32, name="gain_sb")
        bias_sb = keep.tile([P, N_TILES], F32, name="bias_sb")
        cart = [keep.tile([P, S], F32, name=f"cart{i}") for i in range(PACK)]
        wgs_sb = keep.tile([P, S], F32, name="wgs_sb")
        wgt_sb = keep.tile([P, M], F32, name="wgt_sb")
        halves = [(0, BANK), (BANK, 2 * BANK)]
        pile_sb = [keep.tile([P, PACK, BANK], F32, name=f"pile{c}") for c in range(2)]
        wt_raw = keep.tile([P, PACK, N], F32, name="wt_raw")
        wd_codes = keep.tile([P, 2 * N], U8, name="wd_codes", align_bytes=64)

        def load_w1(a):
            rows = w1[a * P * PACK : (a + 1) * P * PACK, :]
            nc.sync.dma_start(out=w1_raw[a][:], in_=rows.rearrange("(p j) c -> p j c", j=PACK))

        def load_tab(a):
            nc.sync.dma_start(out=tab[a][:].bitcast(I32), in_=tab_words[a].rearrange("p t i -> p (t i)").bitcast(I32))

        cart_rows = cartoon.rearrange("(p i) j -> p i j", i=PACK)
        pile_rows = pile.rearrange("(p i) m -> p i m", i=PACK)

        nc.sync.dma_start(idx[:], offs)
        load_tab_scales(nc.scalar, 2)
        load_tab_scales(nc.scalar, 3)
        load_tab(0)
        load_tab_scales(nc.sync, 0)
        load_tab_scales(nc.sync, 1)
        load_w1(0)
        load_w1(1)
        load_tab(1)
        nc.sync.dma_start(out=gain_sb[:], in_=gain.rearrange("(p i) -> p i", i=PACK))
        nc.sync.dma_start(idx2[:], offs2)
        load_w1(2)
        load_tab(2)
        for a, b in halves:
            nc.sync.dma_start(out=cart[0][:, a:b], in_=cart_rows[:, 0, a:b])
            nc.sync.dma_start(out=wgs_sb[:, a:b], in_=wgs[:, a:b])
        nc.sync.dma_start(out=cart[1][:], in_=cart_rows[:, 1, :])
        nc.sync.dma_start(idx3[:], offs3)
        nc.sync.dma_start(out=wgt_sb[:], in_=wgt)
        for i in range(2, PACK):
            nc.sync.dma_start(out=cart[i][:], in_=cart_rows[:, i, :])
        nc.sync.dma_start(out=wt_raw[:], in_=wt.rearrange("(p j) n -> p j n", j=PACK))
        for c, (a, b) in enumerate(halves):
            nc.sync.dma_start(out=pile_sb[c][:], in_=pile_rows[:, :, a:b])
        nc.sync.dma_start(out=wd_codes[:].bitcast(I32), in_=wd_words[0].bitcast(I32))
        for q in range(4):
            nc.sync.dma_start(
                out=wd_sc[32 * q : 32 * q + 4, :].bitcast(I32), in_=wd_scales[0, 4 * q : 4 * q + 4, :].bitcast(I32)
            )
        with nc.allow_non_contiguous_dma(reason="one bias value for each partition and tile of 128 rows"):
            nc.sync.dma_start(out=bias_sb[:], in_=bias.rearrange("(c p) -> p c", p=P))

        v_codes = [keep.tile([P, S], U32, name=f"v_codes{a}", align_bytes=64) for a in range(PASSES - 1)]
        v_sc = keep.tile([P, S], U8, name="v_sc", align_bytes=64)
        w1_codes = [keep.tile([P, H], U32, name=f"w1_codes{a}", align_bytes=64) for a in range(PASSES)]
        w1_sc = [keep.tile([P, H], U8, name=f"w1_sc{a}", align_bytes=64) for a in range(PASSES)]

        nc.vector.tensor_copy(v_codes[0][:], tab[0][:].indirect(idx[:]))
        for q in range(4):
            live = slice(32 * q, 32 * q + 4 * PASSES)
            nc.vector.tensor_copy(tab_sc[live, :].bitcast(I32), tab_sc_rows[live, :])
        nc.vector.tensor_copy(v_sc[:], tab_sc[:].indirect(idx[:]))
        for a in range(PASSES):
            grouped = keep.tile([P, H * PACK], BF16, name=f"w1_grouped{a}", align_bytes=64)
            dst = grouped[:].rearrange("p (i m j) -> p m j i", i=PACK, j=PACK)
            src = w1_raw[a][:].rearrange("p j (m i) -> p m j i", i=PACK)
            share = SCALAR_SHARE[a]
            nc.scalar.copy(out=dst[:, :share], in_=src[:, :share])
            if share < P:
                nc.vector.tensor_copy(out=dst[:, share:], in_=src[:, share:])
            nc.vector.quantize_mx(out=w1_codes[a][:].bitcast(E4M3X4), scales=w1_sc[a][:], in_=grouped[:])
            if a == 0:
                nc.vector.tensor_copy(v_codes[1][:], tab[1][:].indirect(idx[:]))
        v_codes.append(keep.tile([P, S], U32, name="v_codes2", tag="w1_grouped2", align_bytes=64))
        for c0, c1 in halves:
            nc.vector.tensor_copy(v_codes[2][:, c0:c1], tab[2][:].indirect(entries(idx, c0, c1)))

        def knots(i, c0, c1):
            acc = psum.tile([P, BANK], F32, name="acc", bufs=5)
            for a in range(PASSES):
                nc.tensor.matmul_mx(
                    out=acc[:, : c1 - c0],
                    lhsT=w1_codes[a][:, i * P : (i + 1) * P].bitcast(E4M3X4),
                    lhsT_scale=w1_sc[a][:, i * P : (i + 1) * P],
                    rhs=v_codes[a][:, c0:c1].bitcast(E4M3X4),
                    rhs_scale=v_sc[4 * a :, c0:c1],
                    start=(a == 0),
                    stop=(a == PASSES - 1),
                )
            return acc[:, : c1 - c0]

        def deviation_on_vector(h, i, c0, c1):
            acc = knots(i, c0, c1)
            diff = ring.tile([P, BANK], F32, name="stage_a")
            nc.vector.tensor_tensor(diff[:, : c1 - c0], acc, cart[i][:, c0:c1], ALU.subtract)
            size = ring.tile([P, BANK], F32, name="stage_b")
            nc.scalar.activation(out=size[:, : c1 - c0], in_=diff[:, : c1 - c0], func=ACT.Abs)
            nc.scalar.activation(out=h[:, c0:c1], in_=size[:, : c1 - c0], func=ACT.Copy, scale=gain_sb[:, i : i + 1])

        def deviation_on_tensor(h, i, c0, c1):
            acc = knots(i, c0, c1)
            blocks = range((c1 - c0) // P)
            negated = ring.tile([P, BANK], F32, name="stage_a")
            nc.scalar.activation(out=negated[:], in_=acc, func=ACT.Copy, scale=-1.0)
            turned = psum.tile([P, BANK], F32, name="turn")
            for b in blocks:
                nc.tensor.matmul(
                    turned[:, b * P : (b + 1) * P], negated[:, b * P : (b + 1) * P], ident[:],
                    start=True, stop=False, is_transpose=True,
                )
                nc.tensor.matmul(
                    turned[:, b * P : (b + 1) * P], cart[i][:, c0 + b * P : c0 + (b + 1) * P], ident[:],
                    start=False, stop=True, is_transpose=True,
                )
            size = ring.tile([P, BANK], F32, name="stage_b")
            nc.scalar.activation(out=size[:], in_=turned[:], func=ACT.Abs)
            back = psum.tile([P, BANK], F32, name="turn")
            for b in blocks:
                nc.tensor.transpose(back[:, b * P : (b + 1) * P], size[:, b * P : (b + 1) * P], ident[:])
            nc.scalar.activation(out=h[:, c0:c1], in_=back[:], func=ACT.Copy, scale=gain_sb[:, i : i + 1])

        x = [keep.tile([P, PACK, BANK], F32, name=f"x{c}") for c in range(2)]
        for i in range(PACK):
            h = keep.tile([P, S], F32, name=f"h{i}", align_bytes=64)
            page = pages[i % 2]
            if i == 0:
                pieces = [(0, 256), (256, 1024)]
                for c0, c1 in [(0, 256), (256, 512), (512, 1024)]:
                    deviation_on_vector(h, i, c0, c1)
            else:
                pieces = halves if i == 1 else [(0, S)]
                for c0, c1 in halves:
                    deviation_on_tensor(h, i, c0, c1)
            for c0, c1 in pieces:
                nc.vector.tensor_tensor(page[:].indirect(entries(idx2, c0, c1)), h[:, c0:c1], wgs_sb[:, c0:c1], ALU.mult)
            for c, (c0, c1) in enumerate(halves):
                nc.vector.tensor_tensor(x[c][:, i, :], page[:].indirect(entries(idx3, c0, c1)), wgt_sb[:, c0:c1], ALU.mult)

        wt_grouped = keep.tile([P, N * PACK], BF16, name="wt_grouped", tag="h3", align_bytes=64)
        nc.scalar.copy(
            out=wt_grouped[:].rearrange("p (c e j) -> p c j e", e=4, j=PACK),
            in_=wt_raw[:].rearrange("p j (c e) -> p c j e", e=4),
        )
        wt_codes = keep.tile([P, N], U32, name="wt_codes", align_bytes=64)
        wt_sc = keep.tile([P, N], U8, name="wt_sc", align_bytes=64)
        for n0, n1 in ((0, BANK), (BANK, N)):
            nc.vector.quantize_mx(
                out=wt_codes[:, n0:n1].bitcast(E4M3X4), scales=wt_sc[:, n0:n1], in_=wt_grouped[:, PACK * n0 : PACK * n1]
            )

        z_codes, z_sc = [], []
        for c in range(2):
            z = ring.tile([P, BANK * PACK], BF16, name="z", align_bytes=64)
            nc.vector.tensor_tensor(
                z[:].rearrange("p (c e i) -> p c i e", e=4, i=PACK),
                x[c][:].rearrange("p i (c e) -> p c i e", e=4),
                pile_sb[c][:].rearrange("p i (c e) -> p c i e", e=4),
                ALU.min,
            )
            z_codes.append(ring.tile([P, BANK], U32, name="z_codes", align_bytes=64))
            z_sc.append(ring.tile([P, BANK], U8, name="z_sc", align_bytes=64))
            nc.vector.quantize_mx(out=z_codes[c][:].bitcast(E4M3X4), scales=z_sc[c][:], in_=z[:])

        def bend(c, n):
            pattern = psum.tile([P, BANK], F32, name="turn")
            nc.tensor.matmul_mx(
                out=pattern[:],
                lhsT=wt_codes[:, n * P : (n + 1) * P].bitcast(E4M3X4),
                lhsT_scale=wt_sc[:, n * P : (n + 1) * P],
                rhs=z_codes[c][:].bitcast(E4M3X4),
                rhs_scale=z_sc[c][:],
                start=True,
                stop=True,
            )
            result = ring.tile([P, BANK], F32, name="result", bufs=2 * N_TILES)
            nc.scalar.activation(out=result[:], in_=pattern[:], func=ACT.Tanh, bias=bias_sb[:, n : n + 1])
            return result

        def finish(c, n, result):
            density = psum.tile([P, BANK], F32, name="acc", bufs=5)
            nc.tensor.matmul_mx(
                out=density[:],
                lhsT=wd_codes[:, 2 * n * P : 2 * (n + 1) * P].bitcast(E2M1X4),
                lhsT_scale=wd_sc[:, n * P : (n + 1) * P],
                rhs=z_codes[c][:].bitcast(E4M3X4),
                rhs_scale=z_sc[c][:],
                start=True,
                stop=True,
            )
            nc.vector.tensor_tensor(result[:], density[:], result[:], ALU.add)
            c0, c1 = halves[c]
            nc.sync.dma_start(out=out[n * P : (n + 1) * P, c0:c1], in_=result[:])

        results = [bend(0, n) for n in range(N_TILES)]
        for n in range(N_TILES):
            finish(0, n, results[n])
        for n in range(N_TILES):
            finish(1, n, bend(1, n))
